import numpy as np
import ml_dtypes

BF16 = ml_dtypes.bfloat16


def bf(x):
    return np.asarray(x, np.float32).astype(BF16)


def f32(x):
    return np.asarray(x, np.float32)


def f64(x):
    return np.asarray(x).astype(np.float64)


def striped(idx):
    return np.tile(idx.reshape(-1, 16).T, (8, 1))


S, K, M, N, E, Q = 512, 128, 128, 384, 4, 96


def setup_inputs():
    return {"base": bf(np.random.standard_normal((M, S))), "x": bf(np.random.standard_normal((K, N))), "w": bf(np.random.standard_normal((E, K, M)) / np.sqrt(K)), "b": f32(0.5 * np.random.standard_normal((M, 1))), "offs": striped(np.random.permutation(S)[:N])}


def reference(base, x, w, b, offs):
    idx = offs[:16].T.reshape(-1)
    z = f64(base).copy()
    for e in range(E):
        z[:, idx[e * Q : (e + 1) * Q]] = f64(w)[e].T @ f64(x)[:, e * Q : (e + 1) * Q]
    return z + f64(b)

@@ -1,0 +1,53 @@
+import concourse.mybir as mybir
+from concourse.masks import make_identity
+
+BF16, F32, U16 = mybir.dt.bfloat16, mybir.dt.float32, mybir.dt.uint16
+ADD = mybir.AluOpType.add
+
+P = 128
+TOKENS = 512
+ENTRIES = 384
+EXPERTS = 4
+PIECE = ENTRIES // EXPERTS
+PIECE_COLS = PIECE // 16
+
+FLOPS = 2 * P * P * ENTRIES
+
+
+def tile_scatter_matmul_kernel(tc, base, x, w, b, offs, out):
+    nc = tc.nc
+    with (
+        tc.tile_pool(name="held", bufs=1) as held,
+        tc.psum_pool(name="psum", bufs=1) as psum,
+    ):
+        offsets = held.tile([P, ENTRIES // 16], U16, name="offsets")
+        base_sb = held.tile([P, TOKENS], BF16, name="base_sb")
+        x_sb = held.tile([P, ENTRIES], BF16, name="x_sb")
+        w_sb = held.tile([P, EXPERTS, P], BF16, name="w_sb")
+        bias = held.tile([P, 1], F32, name="bias")
+        ident = held.tile([P, P], BF16, name="ident")
+        result = held.tile([P, TOKENS], F32, name="result")
+        window = psum.tile([P, TOKENS], F32, name="window")
+
+        nc.sync.dma_start(offsets[:], offs)
+        nc.scalar.dma_start(base_sb[:], base)
+        nc.gpsimd.dma_start(bias[:], b)
+        nc.sync.dma_start(w_sb[:], w.rearrange("e k m -> k e m"))
+        nc.scalar.dma_start(x_sb[:], x)
+        make_identity(nc, ident[:])
+
+        nc.tensor.matmul(window[:], ident[:], base_sb[:], start=True, stop=True)
+
+        for e in range(EXPERTS):
+            nc.tensor.matmul(
+                window[:].indirect(offsets[:, e * PIECE_COLS : (e + 1) * PIECE_COLS]),
+                w_sb[:, e, :],
+                x_sb[:, e * PIECE : (e + 1) * PIECE],
+                start=True,
+                stop=True,
+            )
+
+        nc.vector.tensor_scalar(
+            out=result[:], in0=window[:], scalar1=bias[:, 0:1], scalar2=None, op0=ADD
+        )
+        nc.sync.dma_start(out, result[:])

@@ -29,12 +29,14 @@ def tile_scatter_matmul_kernel(tc, base, x, w, b, offs, out):
         result = held.tile([P, TOKENS], F32, name="result")
         window = psum.tile([P, TOKENS], F32, name="window")
 
+        make_identity(nc, ident[:])
         nc.sync.dma_start(offsets[:], offs)
         nc.scalar.dma_start(base_sb[:], base)
-        nc.gpsimd.dma_start(bias[:], b)
-        nc.sync.dma_start(w_sb[:], w.rearrange("e k m -> k e m"))
         nc.scalar.dma_start(x_sb[:], x)
-        make_identity(nc, ident[:])
+        for e in range(EXPERTS):
+            queue = nc.sync if e % 2 == 0 else nc.scalar
+            queue.dma_start(w_sb[:, e, :], w[e])
+        nc.sync.dma_start(bias[:], b)
 
         nc.tensor.matmul(window[:], ident[:], base_sb[:], start=True, stop=True)
 

@@ -11,6 +11,8 @@ EXPERTS = 4
 PIECE = ENTRIES // EXPERTS
 PIECE_COLS = PIECE // 16
 
+WARM_UP = 12
+
 FLOPS = 2 * P * P * ENTRIES
 
 
@@ -30,6 +32,12 @@ def tile_scatter_matmul_kernel(tc, base, x, w, b, offs, out):
         window = psum.tile([P, TOKENS], F32, name="window")
 
         make_identity(nc, ident[:])
+
+        zeros = held.tile([P, P], BF16, name="zeros")
+        idle_bank = psum.tile([P, P], F32, name="idle_bank")
+        nc.vector.memset(zeros[:], 0.0)
+        for i in range(WARM_UP):
+            nc.tensor.matmul(idle_bank[:], zeros[:], zeros[:], start=True, stop=True)
         nc.sync.dma_start(offsets[:], offs)
         nc.scalar.dma_start(base_sb[:], base)
         nc.scalar.dma_start(x_sb[:], x)

@@ -6,6 +6,7 @@ ADD = mybir.AluOpType.add
 
 P = 128
 TOKENS = 512
+HALF = TOKENS // 2
 ENTRIES = 384
 EXPERTS = 4
 PIECE = ENTRIES // EXPERTS
@@ -57,7 +58,10 @@ def tile_scatter_matmul_kernel(tc, base, x, w, b, offs, out):
                 stop=True,
             )
 
-        nc.vector.tensor_scalar(
-            out=result[:], in0=window[:], scalar1=bias[:, 0:1], scalar2=None, op0=ADD
-        )
-        nc.sync.dma_start(out, result[:])
+        for half, queue in enumerate((nc.sync, nc.scalar)):
+            columns = slice(half * HALF, (half + 1) * HALF)
+            nc.vector.tensor_scalar(
+                out=result[:, columns], in0=window[:, columns],
+                scalar1=bias[:, 0:1], scalar2=None, op0=ADD,
+            )
+            queue.dma_start(out[:, columns], result[:, columns])

@@ -6,7 +6,6 @@ ADD = mybir.AluOpType.add
 
 P = 128
 TOKENS = 512
-HALF = TOKENS // 2
 ENTRIES = 384
 EXPERTS = 4
 PIECE = ENTRIES // EXPERTS
@@ -42,9 +41,9 @@ def tile_scatter_matmul_kernel(tc, base, x, w, b, offs, out):
         nc.sync.dma_start(offsets[:], offs)
         nc.scalar.dma_start(base_sb[:], base)
         nc.scalar.dma_start(x_sb[:], x)
-        for e in range(EXPERTS):
-            queue = nc.sync if e % 2 == 0 else nc.scalar
-            queue.dma_start(w_sb[:, e, :], w[e])
+        w_by_k = w.rearrange("e k m -> k e m")
+        nc.sync.dma_start(w_sb[:, :2, :], w_by_k[:, :2, :])
+        nc.scalar.dma_start(w_sb[:, 2:, :], w_by_k[:, 2:, :])
         nc.sync.dma_start(bias[:], b)
 
         nc.tensor.matmul(window[:], ident[:], base_sb[:], start=True, stop=True)
@@ -58,10 +57,7 @@ def tile_scatter_matmul_kernel(tc, base, x, w, b, offs, out):
                 stop=True,
             )
 
-        for half, queue in enumerate((nc.sync, nc.scalar)):
-            columns = slice(half * HALF, (half + 1) * HALF)
-            nc.vector.tensor_scalar(
-                out=result[:, columns], in0=window[:, columns],
-                scalar1=bias[:, 0:1], scalar2=None, op0=ADD,
-            )
-            queue.dma_start(out[:, columns], result[:, columns])
+        nc.vector.tensor_scalar(
+            out=result[:], in0=window[:], scalar1=bias[:, 0:1], scalar2=None, op0=ADD
+        )
+        nc.sync.dma_start(out, result[:])

@@ -12,7 +12,7 @@ PIECE = ENTRIES // EXPERTS
 PIECE_COLS = PIECE // 16
 
 WARM_UP = 12
-
+ROW_START = 256
 FLOPS = 2 * P * P * ENTRIES
 
 
@@ -22,13 +22,13 @@ def tile_scatter_matmul_kernel(tc, base, x, w, b, offs, out):
         tc.tile_pool(name="held", bufs=1) as held,
         tc.psum_pool(name="psum", bufs=1) as psum,
     ):
-        offsets = held.tile([P, ENTRIES // 16], U16, name="offsets")
-        base_sb = held.tile([P, TOKENS], BF16, name="base_sb")
-        x_sb = held.tile([P, ENTRIES], BF16, name="x_sb")
-        w_sb = held.tile([P, EXPERTS, P], BF16, name="w_sb")
-        bias = held.tile([P, 1], F32, name="bias")
+        offsets = held.tile([P, ENTRIES // 16], U16, name="offsets", align_bytes=ROW_START)
+        base_sb = held.tile([P, TOKENS], BF16, name="base_sb", align_bytes=ROW_START)
+        x_sb = held.tile([P, ENTRIES], BF16, name="x_sb", align_bytes=ROW_START)
+        w_sb = held.tile([P, EXPERTS, P], BF16, name="w_sb", align_bytes=ROW_START)
+        bias = held.tile([P, 1], F32, name="bias", align_bytes=ROW_START)
         ident = held.tile([P, P], BF16, name="ident")
-        result = held.tile([P, TOKENS], F32, name="result")
+        result = held.tile([P, TOKENS], F32, name="result", align_bytes=ROW_START)
         window = psum.tile([P, TOKENS], F32, name="window")
 
         make_identity(nc, ident[:])
@@ -38,6 +38,7 @@ def tile_scatter_matmul_kernel(tc, base, x, w, b, offs, out):
         nc.vector.memset(zeros[:], 0.0)
         for i in range(WARM_UP):
             nc.tensor.matmul(idle_bank[:], zeros[:], zeros[:], start=True, stop=True)
+
         nc.sync.dma_start(offsets[:], offs)
         nc.scalar.dma_start(base_sb[:], base)
         nc.scalar.dma_start(x_sb[:], x)

@@ -11,7 +11,7 @@ EXPERTS = 4
 PIECE = ENTRIES // EXPERTS
 PIECE_COLS = PIECE // 16
 
-WARM_UP = 12
+WARM_UP = 10
 ROW_START = 256
 FLOPS = 2 * P * P * ENTRIES
 

@@ -10,6 +10,7 @@ ENTRIES = 384
 EXPERTS = 4
 PIECE = ENTRIES // EXPERTS
 PIECE_COLS = PIECE // 16
+BLOCK = 32
 
 WARM_UP = 10
 ROW_START = 256
@@ -26,7 +27,8 @@ def tile_scatter_matmul_kernel(tc, base, x, w, b, offs, out):
         base_sb = held.tile([P, TOKENS], BF16, name="base_sb", align_bytes=ROW_START)
         x_sb = held.tile([P, ENTRIES], BF16, name="x_sb", align_bytes=ROW_START)
         w_sb = held.tile([P, EXPERTS, P], BF16, name="w_sb", align_bytes=ROW_START)
-        bias = held.tile([P, 1], F32, name="bias", align_bytes=ROW_START)
+        b_blocks = held.tile([P, BLOCK], F32, name="b_blocks", align_bytes=ROW_START)
+        bias = held.tile([P, BLOCK], F32, name="bias", align_bytes=ROW_START)
         ident = held.tile([P, P], BF16, name="ident")
         result = held.tile([P, TOKENS], F32, name="result", align_bytes=ROW_START)
         window = psum.tile([P, TOKENS], F32, name="window")
@@ -45,7 +47,10 @@ def tile_scatter_matmul_kernel(tc, base, x, w, b, offs, out):
         w_by_k = w.rearrange("e k m -> k e m")
         nc.sync.dma_start(w_sb[:, :2, :], w_by_k[:, :2, :])
         nc.scalar.dma_start(w_sb[:, 2:, :], w_by_k[:, 2:, :])
-        nc.sync.dma_start(bias[:], b)
+
+        nc.vector.memset(b_blocks[:], 0.0)
+        nc.sync.dma_start(b_blocks[::BLOCK, :], b.rearrange("(a i) o -> a (i o)", i=BLOCK))
+        nc.vector.transpose(bias[:], b_blocks[:])
 
         nc.tensor.matmul(window[:], ident[:], base_sb[:], start=True, stop=True)
 

@@ -41,16 +41,16 @@ def tile_scatter_matmul_kernel(tc, base, x, w, b, offs, out):
         for i in range(WARM_UP):
             nc.tensor.matmul(idle_bank[:], zeros[:], zeros[:], start=True, stop=True)
 
-        nc.sync.dma_start(offsets[:], offs)
-        nc.scalar.dma_start(base_sb[:], base)
-        nc.scalar.dma_start(x_sb[:], x)
-        w_by_k = w.rearrange("e k m -> k e m")
-        nc.sync.dma_start(w_sb[:, :2, :], w_by_k[:, :2, :])
-        nc.scalar.dma_start(w_sb[:, 2:, :], w_by_k[:, 2:, :])
-
         nc.vector.memset(b_blocks[:], 0.0)
-        nc.sync.dma_start(b_blocks[::BLOCK, :], b.rearrange("(a i) o -> a (i o)", i=BLOCK))
+        nc.scalar.dma_start(b_blocks[::BLOCK, :], b.rearrange("(a i) o -> a (o i)", i=BLOCK))
         nc.vector.transpose(bias[:], b_blocks[:])
+
+        w_by_k = w.rearrange("e k m -> k e m")
+        nc.sync.dma_start(base_sb[:], base)
+        nc.sync.dma_start(x_sb[:], x)
+        nc.sync.dma_start(offsets[:], offs)
+        nc.sync.dma_start(w_sb[:, :2, :], w_by_k[:, :2, :])
+        nc.sync.dma_start(w_sb[:, 2:, :], w_by_k[:, 2:, :])
 
         nc.tensor.matmul(window[:], ident[:], base_sb[:], start=True, stop=True)
 

@@ -12,7 +12,7 @@ PIECE = ENTRIES // EXPERTS
 PIECE_COLS = PIECE // 16
 BLOCK = 32
 
-WARM_UP = 10
+WARM_UP = 8
 ROW_START = 256
 FLOPS = 2 * P * P * ENTRIES
 

import concourse.mybir as mybir
from concourse.masks import make_identity

BF16, F32, U16 = mybir.dt.bfloat16, mybir.dt.float32, mybir.dt.uint16
ADD = mybir.AluOpType.add

P = 128
TOKENS = 512
ENTRIES = 384
EXPERTS = 4
PIECE = ENTRIES // EXPERTS
PIECE_COLS = PIECE // 16
BLOCK = 32

WARM_UP = 8
ROW_START = 256
FLOPS = 2 * P * P * ENTRIES


def tile_scatter_matmul_kernel(tc, base, x, w, b, offs, out):
    nc = tc.nc
    with (
        tc.tile_pool(name="held", bufs=1) as held,
        tc.psum_pool(name="psum", bufs=1) as psum,
    ):
        offsets = held.tile([P, ENTRIES // 16], U16, name="offsets", align_bytes=ROW_START)
        base_sb = held.tile([P, TOKENS], BF16, name="base_sb", align_bytes=ROW_START)
        x_sb = held.tile([P, ENTRIES], BF16, name="x_sb", align_bytes=ROW_START)
        w_sb = held.tile([P, EXPERTS, P], BF16, name="w_sb", align_bytes=ROW_START)
        b_blocks = held.tile([P, BLOCK], F32, name="b_blocks", align_bytes=ROW_START)
        bias = held.tile([P, BLOCK], F32, name="bias", align_bytes=ROW_START)
        ident = held.tile([P, P], BF16, name="ident")
        result = held.tile([P, TOKENS], F32, name="result", align_bytes=ROW_START)
        window = psum.tile([P, TOKENS], F32, name="window")

        make_identity(nc, ident[:])

        zeros = held.tile([P, P], BF16, name="zeros")
        idle_bank = psum.tile([P, P], F32, name="idle_bank")
        nc.vector.memset(zeros[:], 0.0)
        for i in range(WARM_UP):
            nc.tensor.matmul(idle_bank[:], zeros[:], zeros[:], start=True, stop=True)

        nc.vector.memset(b_blocks[:], 0.0)
        nc.scalar.dma_start(b_blocks[::BLOCK, :], b.rearrange("(a i) o -> a (o i)", i=BLOCK))
        nc.vector.transpose(bias[:], b_blocks[:])

        w_by_k = w.rearrange("e k m -> k e m")
        nc.sync.dma_start(base_sb[:], base)
        nc.sync.dma_start(x_sb[:], x)
        nc.sync.dma_start(offsets[:], offs)
        nc.sync.dma_start(w_sb[:, :2, :], w_by_k[:, :2, :])
        nc.sync.dma_start(w_sb[:, 2:, :], w_by_k[:, 2:, :])

        nc.tensor.matmul(window[:], ident[:], base_sb[:], start=True, stop=True)

        for e in range(EXPERTS):
            nc.tensor.matmul(
                window[:].indirect(offsets[:, e * PIECE_COLS : (e + 1) * PIECE_COLS]),
                w_sb[:, e, :],
                x_sb[:, e * PIECE : (e + 1) * PIECE],
                start=True,
                stop=True,
            )

        nc.vector.tensor_scalar(
            out=result[:], in0=window[:], scalar1=bias[:, 0:1], scalar2=None, op0=ADD
        )
        nc.sync.dma_start(out, result[:])
